import numpy as np
import ml_dtypes


def mxq(x, axis, fmt="e4m3"):
    dtype, down = {"e4m3": (ml_dtypes.float8_e4m3fn, 7), "e5m2": (ml_dtypes.float8_e5m2, 14)}[fmt]
    v = np.moveaxis(np.asarray(x, np.float32).astype(ml_dtypes.bfloat16).astype(np.float64), axis, -1)
    blocks = v.reshape(v.shape[:-1] + (-1, 32))
    amax = np.abs(blocks).max(-1, keepdims=True)
    byte = np.maximum(np.where(amax > 0, np.frexp(amax)[1] - 1 + 127, 0) - down, 1)
    scale = np.exp2(byte - 127.0)
    codes = (blocks / scale).astype(np.float32).astype(dtype).astype(np.float64)
    return np.moveaxis((codes * scale).reshape(v.shape), -1, axis)


WIDE = False


def mx_kscale(k):
    if not WIDE:
        return np.ones(k)
    levels = np.array([10, -10, 5, -5, 0])
    if k % 512:
        return np.exp2(np.random.permutation(np.resize(levels, k // 32))).repeat(32)
    a = np.empty((k // 512, 16))
    for p in range(k // 512):
        a[p, :8] = np.random.permutation(np.resize(levels, 8))
        for g in range(8):
            far = levels[np.abs(levels - a[p, g]) >= 10]
            a[p, g + 8] = far[np.random.randint(len(far))]
    return np.exp2(a.ravel()).repeat(32)


def f64(x):
    return np.asarray(x).astype(np.float64)


def striped(idx):
    return np.tile(np.asarray(idx).reshape(-1, 16).T, (8, 1)).astype(np.uint16)


def unstriped(offs):
    return offs[:16].T.reshape(-1).astype(np.int64)


N, T, D, H, M, G, K = 512, 2048, 512, 512, 128, 256, 4


def setup_inputs():
    n = np.random.standard_normal
    s = mx_kscale(D)[:, None]
    u = mx_kscale(H)[:, None]
    return {
        "xT": (n((D, T)) * s).astype(np.float32),
        "w1": (n((D, H)) / np.sqrt(D) / s * u[:, 0]).astype(np.float32),
        "w2": (n((H, M)) / np.sqrt(H * K) / u).astype(np.float32),
        "offs": striped(np.random.permutation(T)[:N]),
        "offs2": striped(np.random.randint(0, N, G * K)),
    }


def reference(xT, w1, w2, offs, offs2):
    a = mxq(f64(w1), 0, "e4m3").T @ mxq(f64(xT)[:, unstriped(offs)], 0, "e4m3")
    h = np.maximum(a, 0.0)
    e = h[:, unstriped(offs2)].reshape(H, G, K).sum(-1)
    return mxq(f64(w2), 0, "e4m3").T @ mxq(e, 0, "e4m3")

@@ -1,0 +1,146 @@
+import concourse.mybir as mybir
+
+P = 128
+PACK = 4
+N, T, D, H, M, G, K = 512, 2048, 512, 512, 128, 256, 4
+FLOPS = 2 * D * H * N + 2 * H * M * G
+
+F32 = mybir.dt.float32
+BF16 = mybir.dt.bfloat16
+U32 = mybir.dt.uint32
+U16 = mybir.dt.uint16
+U8 = mybir.dt.uint8
+FP8X4 = mybir.dt.float8_e4m3fn_x4
+ADD = mybir.AluOpType.add
+RELU = mybir.ActivationFunctionType.Relu
+
+H_WINDOW = N + 8
+HALF = N // 2
+CHUNKS = ((0, 128, "gpsimd"), (128, 64, "gpsimd"), (192, 64, "vector"))
+
+
+def tile_attend_hop_kernel(tc, xT, w1, w2, offs, offs2, out):
+    nc = tc.nc
+    with (
+        tc.tile_pool(name="held", bufs=1) as held,
+        tc.psum_pool(name="psum", bufs=1) as psum,
+    ):
+        list1 = held.tile([P, N // 16], U16, name="list1")
+        list2 = held.tile([P, G * K // 16], U16, name="list2")
+
+        x_rows = xT.rearrange("(p t) n -> t p n", t=PACK)
+        x_raw = [held.tile([P, T], F32, name=f"x_raw{t}") for t in range(PACK)]
+        w1_raw = held.tile([P, PACK, H], F32, name="w1_raw")
+        w2_raw = held.tile([P, PACK, M], F32, name="w2_raw")
+        nc.sync.dma_start(x_raw[0][:], x_rows[0])
+        nc.sync.dma_start(list1[:], offs)
+        nc.sync.dma_start(x_raw[1][:], x_rows[1])
+        nc.sync.dma_start(x_raw[2][:], x_rows[2])
+        nc.sync.dma_start(x_raw[3][:], x_rows[3])
+        nc.sync.dma_start(w1_raw[:], w1.rearrange("(p j) c -> p j c", j=PACK))
+        nc.sync.dma_start(list2[:], offs2)
+        nc.sync.dma_start(w2_raw[:], w2.rearrange("(p j) m -> p j m", j=PACK))
+
+        h = []
+        for t in range(PACK):
+            h_t = held.tile([P, H_WINDOW], F32, name=f"h{t}")
+            nc.gpsimd.memset(h_t[:, N:], 0.0)
+            h.append(h_t)
+
+        x_grouped = held.tile([P, N, PACK], BF16, align_bytes=64, name="x_grouped")
+        x_codes = held.tile([P, N], U32, align_bytes=64, name="x_codes")
+        x_scales = held.tile([P, N], U8, align_bytes=64, name="x_scales")
+        for t in range(PACK):
+            nc.vector.tensor_copy(x_grouped[:, :, t], x_raw[t][:].indirect(list1[:]))
+        for s in range(2):
+            cols = slice(s * HALF, (s + 1) * HALF)
+            nc.vector.quantize_mx(
+                out=x_codes[:, cols].bitcast(FP8X4),
+                scales=x_scales[:, cols],
+                in_=x_grouped[:, cols, :].rearrange("p n t -> p (n t)"),
+            )
+
+        w1_by_t = w1_raw[:].rearrange("p j (m t) -> p t m j", t=PACK)
+        bank = psum.tile([P, HALF], F32, name="bank0a")
+        bank_b = psum.tile([P, HALF], F32, name="bank0b")
+        for t in range(PACK):
+            w_grouped = held.tile([P, P, PACK], BF16, align_bytes=64, name=f"w_grouped{t}")
+            w_codes = held.tile([P, P], U32, align_bytes=64, name=f"w_codes{t}")
+            w_scales = held.tile([P, P], U8, align_bytes=64, name=f"w_scales{t}")
+            if t % 2 == 0:
+                nc.vector.tensor_copy(w_grouped[:], w1_by_t[:, t])
+            else:
+                nc.scalar.copy(w_grouped[:], w1_by_t[:, t])
+            nc.vector.quantize_mx(
+                out=w_codes[:].bitcast(FP8X4), scales=w_scales[:], in_=w_grouped[:].rearrange("p m j -> p (m j)")
+            )
+            if t == 0:
+                parts = ((0, HALF, bank), (HALF, N, bank_b))
+            else:
+                bank_t = psum.tile([P, N], F32, name=f"bank{t}")
+                parts = ((0, N, bank_t),)
+            for a, b, acc in parts:
+                nc.tensor.matmul_mx(
+                    out=acc[:],
+                    lhsT=w_codes[:].bitcast(FP8X4),
+                    lhsT_scale=w_scales[:],
+                    rhs=x_codes[:, a:b].bitcast(FP8X4),
+                    rhs_scale=x_scales[:, a:b],
+                    start=True,
+                    stop=True,
+                )
+            for a, b, acc in parts:
+                if t == 0 and a == 0:
+                    nc.vector.tensor_scalar_max(h[t][:, a:b], acc[:], 0.0)
+                else:
+                    nc.scalar.activation(h[t][:, a:b], acc[:], RELU)
+
+        w2_grouped = held.tile([P, M, PACK], BF16, align_bytes=64, name="w2_grouped")
+        w2_codes = held.tile([P, M], U32, align_bytes=64, name="w2_codes")
+        w2_scales = held.tile([P, M], U8, align_bytes=64, name="w2_scales")
+
+        for c, (g0, ng, engine) in enumerate(CHUNKS):
+            picked = held.tile([P, PACK, ng * K], F32, name=f"picked{c}")
+            pairs = held.tile([P, PACK, ng, 2], F32, name=f"pairs{c}")
+            e = held.tile([P, ng, PACK], BF16, align_bytes=64, name=f"e{c}")
+            e_codes = held.tile([P, ng], U32, align_bytes=64, name=f"e_codes{c}")
+            e_scales = held.tile([P, ng], U8, align_bytes=64, name=f"e_scales{c}")
+            where = list2[:, g0 * K // 16 : (g0 + ng) * K // 16]
+            eng = nc.gpsimd if engine == "gpsimd" else nc.vector
+            for t in range(PACK):
+                nc.vector.tensor_copy(picked[:, t, :], h[t][:].indirect(where))
+                four = picked[:, t, :].rearrange("p (g j) -> p g j", j=K)
+                if engine == "gpsimd":
+                    eng.tensor_tensor(pairs[:, t], four[:, :, 0:2], four[:, :, 2:4], ADD)
+            if engine == "vector":
+                with nc.allow_low_precision(reason="the sum is float32 inside the engine and rounded once on the way out"):
+                    nc.vector.tensor_reduce(
+                        out=e[:],
+                        in_=picked[:].rearrange("p t (g j) -> p g t j", j=K),
+                        axis=mybir.AxisListType.X,
+                        op=ADD,
+                    )
+            else:
+                by_g = pairs[:].rearrange("p t g b -> p g t b")
+                eng.tensor_tensor(e[:], by_g[:, :, :, 0], by_g[:, :, :, 1], ADD)
+            if c == 0:
+                nc.scalar.copy(w2_grouped[:], w2_raw[:].rearrange("p j m -> p m j"))
+                nc.vector.quantize_mx(
+                    out=w2_codes[:].bitcast(FP8X4), scales=w2_scales[:], in_=w2_grouped[:].rearrange("p m j -> p (m j)")
+                )
+            nc.vector.quantize_mx(
+                out=e_codes[:].bitcast(FP8X4), scales=e_scales[:], in_=e[:].rearrange("p g t -> p (g t)")
+            )
+            acc = psum.tile([P, ng], F32, name=f"out_bank{c}")
+            nc.tensor.matmul_mx(
+                out=acc[:],
+                lhsT=w2_codes[:].bitcast(FP8X4),
+                lhsT_scale=w2_scales[:],
+                rhs=e_codes[:].bitcast(FP8X4),
+                rhs_scale=e_scales[:],
+                start=True,
+                stop=True,
+            )
+            result = held.tile([P, ng], F32, name=f"result{c}")
+            nc.scalar.copy(result[:], acc[:])
+            nc.sync.dma_start(out[:, g0 : g0 + ng], result[:])

@@ -14,9 +14,10 @@ FP8X4 = mybir.dt.float8_e4m3fn_x4
 ADD = mybir.AluOpType.add
 RELU = mybir.ActivationFunctionType.Relu
 
-H_WINDOW = N + 8
+WINDOW = N + 8
 HALF = N // 2
-CHUNKS = ((0, 128, "gpsimd"), (128, 64, "gpsimd"), (192, 64, "vector"))
+LAST = 64
+EARLY = G - LAST
 
 
 def tile_attend_hop_kernel(tc, xT, w1, w2, offs, offs2, out):
@@ -43,104 +44,119 @@ def tile_attend_hop_kernel(tc, xT, w1, w2, offs, offs2, out):
 
         h = []
         for t in range(PACK):
-            h_t = held.tile([P, H_WINDOW], F32, name=f"h{t}")
+            h_t = held.tile([P, WINDOW], F32, name=f"h{t}")
             nc.gpsimd.memset(h_t[:, N:], 0.0)
             h.append(h_t)
 
+        def quantize(codes, scales, grouped):
+            nc.vector.quantize_mx(out=codes.bitcast(FP8X4), scales=scales, in_=grouped.rearrange("p n t -> p (n t)"))
+
+        def multiply(acc, w, x, cols):
+            nc.tensor.matmul_mx(
+                out=acc,
+                lhsT=w[0][:].bitcast(FP8X4),
+                lhsT_scale=w[1][:],
+                rhs=x[0][:, cols].bitcast(FP8X4),
+                rhs_scale=x[1][:, cols],
+                start=True,
+                stop=True,
+            )
+
+        def mx_tiles(width, name):
+            codes = held.tile([P, width], U32, align_bytes=64, name=f"{name}_codes")
+            scales = held.tile([P, width], U8, align_bytes=64, name=f"{name}_scales")
+            return codes, scales
+
         x_grouped = held.tile([P, N, PACK], BF16, align_bytes=64, name="x_grouped")
-        x_codes = held.tile([P, N], U32, align_bytes=64, name="x_codes")
-        x_scales = held.tile([P, N], U8, align_bytes=64, name="x_scales")
+        x_mx = mx_tiles(N, "x")
         for t in range(PACK):
             nc.vector.tensor_copy(x_grouped[:, :, t], x_raw[t][:].indirect(list1[:]))
         for s in range(2):
             cols = slice(s * HALF, (s + 1) * HALF)
-            nc.vector.quantize_mx(
-                out=x_codes[:, cols].bitcast(FP8X4),
-                scales=x_scales[:, cols],
-                in_=x_grouped[:, cols, :].rearrange("p n t -> p (n t)"),
-            )
+            quantize(x_mx[0][:, cols], x_mx[1][:, cols], x_grouped[:, cols, :])
 
         w1_by_t = w1_raw[:].rearrange("p j (m t) -> p t m j", t=PACK)
-        bank = psum.tile([P, HALF], F32, name="bank0a")
-        bank_b = psum.tile([P, HALF], F32, name="bank0b")
-        for t in range(PACK):
-            w_grouped = held.tile([P, P, PACK], BF16, align_bytes=64, name=f"w_grouped{t}")
-            w_codes = held.tile([P, P], U32, align_bytes=64, name=f"w_codes{t}")
-            w_scales = held.tile([P, P], U8, align_bytes=64, name=f"w_scales{t}")
-            if t % 2 == 0:
-                nc.vector.tensor_copy(w_grouped[:], w1_by_t[:, t])
-            else:
-                nc.scalar.copy(w_grouped[:], w1_by_t[:, t])
-            nc.vector.quantize_mx(
-                out=w_codes[:].bitcast(FP8X4), scales=w_scales[:], in_=w_grouped[:].rearrange("p m j -> p (m j)")
-            )
+        w_grouped = [held.tile([P, P, PACK], BF16, align_bytes=64, name=f"w_grouped{t}") for t in range(PACK)]
+        w_mx = [mx_tiles(P, f"w{t}") for t in range(PACK)]
+
+        def layer1(t):
             if t == 0:
-                parts = ((0, HALF, bank), (HALF, N, bank_b))
+                nc.vector.tensor_copy(w_grouped[t][:], w1_by_t[:, t])
             else:
-                bank_t = psum.tile([P, N], F32, name=f"bank{t}")
-                parts = ((0, N, bank_t),)
-            for a, b, acc in parts:
-                nc.tensor.matmul_mx(
-                    out=acc[:],
-                    lhsT=w_codes[:].bitcast(FP8X4),
-                    lhsT_scale=w_scales[:],
-                    rhs=x_codes[:, a:b].bitcast(FP8X4),
-                    rhs_scale=x_scales[:, a:b],
-                    start=True,
-                    stop=True,
-                )
-            for a, b, acc in parts:
-                if t == 0 and a == 0:
-                    nc.vector.tensor_scalar_max(h[t][:, a:b], acc[:], 0.0)
-                else:
-                    nc.scalar.activation(h[t][:, a:b], acc[:], RELU)
+                nc.scalar.copy(w_grouped[t][:], w1_by_t[:, t])
+            quantize(w_mx[t][0][:], w_mx[t][1][:], w_grouped[t][:])
+            if t == 0:
+                for s in range(2):
+                    cols = slice(s * HALF, (s + 1) * HALF)
+                    acc = psum.tile([P, HALF], F32, name=f"bank0{s}")
+                    multiply(acc[:], w_mx[t], x_mx, cols)
+                    if s == 0:
+                        nc.scalar.activation(h[t][:, cols], acc[:], RELU)
+                    else:
+                        nc.vector.tensor_scalar_max(h[t][:, cols], acc[:], 0.0)
+            else:
+                acc = psum.tile([P, N], F32, name=f"bank{t}")
+                multiply(acc[:], w_mx[t], x_mx, slice(0, N))
+                nc.scalar.activation(h[t][:, 0:N], acc[:], RELU)
 
+        picked = held.tile([P, PACK, G, K], F32, name="picked")
+        pairs = held.tile([P, PACK, G, 2], F32, name="pairs")
+        sums = held.tile([P, PACK, G], F32, name="sums")
+
+        def pick(t, g0, g1):
+            nc.vector.tensor_copy(
+                picked[:, t, g0:g1, :].rearrange("p g j -> p (g j)"),
+                h[t][:].indirect(list2[:, g0 * K // 16 : g1 * K // 16]),
+            )
+
+        def add_pairs(t0, t1, g0, g1):
+            nc.vector.tensor_tensor(
+                pairs[:, t0:t1, g0:g1, :], picked[:, t0:t1, g0:g1, 0:2], picked[:, t0:t1, g0:g1, 2:4], ADD
+            )
+
+        def add_sums(t0, t1, g0, g1):
+            nc.vector.tensor_tensor(
+                sums[:, t0:t1, g0:g1], pairs[:, t0:t1, g0:g1, 0], pairs[:, t0:t1, g0:g1, 1], ADD
+            )
+
+        layer1(0)
+        layer1(1)
+        pick(0, 0, 128)
+        pick(0, 128, G)
+        layer1(2)
+        pick(1, 0, 128)
+        pick(1, 128, G)
+        layer1(3)
         w2_grouped = held.tile([P, M, PACK], BF16, align_bytes=64, name="w2_grouped")
-        w2_codes = held.tile([P, M], U32, align_bytes=64, name="w2_codes")
-        w2_scales = held.tile([P, M], U8, align_bytes=64, name="w2_scales")
+        w2_mx = mx_tiles(M, "w2")
+        nc.scalar.copy(w2_grouped[:], w2_raw[:].rearrange("p j m -> p m j"))
+        pick(2, 0, 128)
+        pick(2, 128, G)
+        quantize(w2_mx[0][:], w2_mx[1][:], w2_grouped[:])
+        add_pairs(0, 2, 0, G)
+        pick(3, 0, 128)
+        add_pairs(2, 3, 0, G)
+        pick(3, 128, EARLY)
+        add_sums(0, 3, 0, G)
+        add_pairs(3, 4, 0, EARLY)
+        e_late = held.tile([P, LAST, PACK], BF16, align_bytes=64, name="e_late")
+        nc.vector.tensor_copy(e_late[:, :, 0:3], sums[:, 0:3, EARLY:G].rearrange("p t g -> p g t"))
+        add_sums(3, 4, 0, EARLY)
+        pick(3, EARLY, G)
 
-        for c, (g0, ng, engine) in enumerate(CHUNKS):
-            picked = held.tile([P, PACK, ng * K], F32, name=f"picked{c}")
-            pairs = held.tile([P, PACK, ng, 2], F32, name=f"pairs{c}")
-            e = held.tile([P, ng, PACK], BF16, align_bytes=64, name=f"e{c}")
-            e_codes = held.tile([P, ng], U32, align_bytes=64, name=f"e_codes{c}")
-            e_scales = held.tile([P, ng], U8, align_bytes=64, name=f"e_scales{c}")
-            where = list2[:, g0 * K // 16 : (g0 + ng) * K // 16]
-            eng = nc.gpsimd if engine == "gpsimd" else nc.vector
-            for t in range(PACK):
-                nc.vector.tensor_copy(picked[:, t, :], h[t][:].indirect(where))
-                four = picked[:, t, :].rearrange("p (g j) -> p g j", j=K)
-                if engine == "gpsimd":
-                    eng.tensor_tensor(pairs[:, t], four[:, :, 0:2], four[:, :, 2:4], ADD)
-            if engine == "vector":
-                with nc.allow_low_precision(reason="the sum is float32 inside the engine and rounded once on the way out"):
-                    nc.vector.tensor_reduce(
-                        out=e[:],
-                        in_=picked[:].rearrange("p t (g j) -> p g t j", j=K),
-                        axis=mybir.AxisListType.X,
-                        op=ADD,
-                    )
-            else:
-                by_g = pairs[:].rearrange("p t g b -> p g t b")
-                eng.tensor_tensor(e[:], by_g[:, :, :, 0], by_g[:, :, :, 1], ADD)
-            if c == 0:
-                nc.scalar.copy(w2_grouped[:], w2_raw[:].rearrange("p j m -> p m j"))
-                nc.vector.quantize_mx(
-                    out=w2_codes[:].bitcast(FP8X4), scales=w2_scales[:], in_=w2_grouped[:].rearrange("p m j -> p (m j)")
-                )
-            nc.vector.quantize_mx(
-                out=e_codes[:].bitcast(FP8X4), scales=e_scales[:], in_=e[:].rearrange("p g t -> p (g t)")
-            )
-            acc = psum.tile([P, ng], F32, name=f"out_bank{c}")
-            nc.tensor.matmul_mx(
-                out=acc[:],
-                lhsT=w2_codes[:].bitcast(FP8X4),
-                lhsT_scale=w2_scales[:],
-                rhs=e_codes[:].bitcast(FP8X4),
-                rhs_scale=e_scales[:],
-                start=True,
-                stop=True,
-            )
-            result = held.tile([P, ng], F32, name=f"result{c}")
+        e_early = held.tile([P, EARLY, PACK], BF16, align_bytes=64, name="e_early")
+        e_mx = [mx_tiles(128, "e0"), mx_tiles(LAST, "e1"), mx_tiles(LAST, "e2")]
+        parts = ((0, 128), (128, EARLY), (EARLY, G))
+        for g0, g1 in parts[:2]:
+            nc.scalar.copy(e_early[:, g0:g1, :], sums[:, :, g0:g1].rearrange("p t g -> p g t"))
+        quantize(e_mx[0][0][:], e_mx[0][1][:], e_early[:, 0:128, :])
+        with nc.allow_low_precision(reason="the engine sums in float32 and rounds once, on the way out"):
+            nc.vector.tensor_reduce(out=e_late[:, :, 3], in_=picked[:, 3, EARLY:G, :], axis=mybir.AxisListType.X, op=ADD)
+        quantize(e_mx[1][0][:], e_mx[1][1][:], e_early[:, 128:EARLY, :])
+        quantize(e_mx[2][0][:], e_mx[2][1][:], e_late[:])
+        for c, (g0, g1) in enumerate(parts):
+            acc = psum.tile([P, g1 - g0], F32, name=f"out_bank{c}")
+            multiply(acc[:], w2_mx, e_mx[c], slice(0, g1 - g0))
+            result = held.tile([P, g1 - g0], F32, name=f"result{c}")
             nc.scalar.copy(result[:], acc[:])
-            nc.sync.dma_start(out[:, g0 : g0 + ng], result[:])
+            nc.sync.dma_start(out[:, g0:g1], result[:])

@@ -81,7 +81,8 @@ def tile_attend_hop_kernel(tc, xT, w1, w2, offs, offs2, out):
 
         def layer1(t):
             if t == 0:
-                nc.vector.tensor_copy(w_grouped[t][:], w1_by_t[:, t])
+                nc.scalar.copy(w_grouped[t][:, 64:], w1_by_t[:, t, 64:])
+                nc.vector.tensor_copy(w_grouped[t][:, :64], w1_by_t[:, t, :64])
             else:
                 nc.scalar.copy(w_grouped[t][:], w1_by_t[:, t])
             quantize(w_mx[t][0][:], w_mx[t][1][:], w_grouped[t][:])
@@ -109,40 +110,36 @@ def tile_attend_hop_kernel(tc, xT, w1, w2, offs, offs2, out):
                 h[t][:].indirect(list2[:, g0 * K // 16 : g1 * K // 16]),
             )
 
-        def add_pairs(t0, t1, g0, g1):
-            nc.vector.tensor_tensor(
-                pairs[:, t0:t1, g0:g1, :], picked[:, t0:t1, g0:g1, 0:2], picked[:, t0:t1, g0:g1, 2:4], ADD
-            )
+        def add(t, g0, g1):
+            nc.gpsimd.tensor_tensor(pairs[:, t, g0:g1, :], picked[:, t, g0:g1, 0:2], picked[:, t, g0:g1, 2:4], ADD)
 
-        def add_sums(t0, t1, g0, g1):
-            nc.vector.tensor_tensor(
-                sums[:, t0:t1, g0:g1], pairs[:, t0:t1, g0:g1, 0], pairs[:, t0:t1, g0:g1, 1], ADD
-            )
+        def finish(t, g0, g1):
+            nc.gpsimd.tensor_tensor(sums[:, t, g0:g1], pairs[:, t, g0:g1, 0], pairs[:, t, g0:g1, 1], ADD)
 
         layer1(0)
         layer1(1)
-        pick(0, 0, 128)
-        pick(0, 128, G)
-        layer1(2)
-        pick(1, 0, 128)
-        pick(1, 128, G)
-        layer1(3)
+        for t in range(3):
+            for g0 in (0, 128):
+                pick(t, g0, g0 + 128)
+                if t == 2:
+                    add(t, g0, g0 + 128)
+            if t < 2:
+                add(t, 0, G)
+            finish(t, 0, G)
+            if t < 2:
+                layer1(t + 2)
         w2_grouped = held.tile([P, M, PACK], BF16, align_bytes=64, name="w2_grouped")
         w2_mx = mx_tiles(M, "w2")
         nc.scalar.copy(w2_grouped[:], w2_raw[:].rearrange("p j m -> p m j"))
-        pick(2, 0, 128)
-        pick(2, 128, G)
         quantize(w2_mx[0][:], w2_mx[1][:], w2_grouped[:])
-        add_pairs(0, 2, 0, G)
         pick(3, 0, 128)
-        add_pairs(2, 3, 0, G)
+        add(3, 0, 128)
+        finish(3, 0, 128)
         pick(3, 128, EARLY)
-        add_sums(0, 3, 0, G)
-        add_pairs(3, 4, 0, EARLY)
+        nc.vector.tensor_reduce(out=sums[:, 3, 128:EARLY], in_=picked[:, 3, 128:EARLY, :], axis=mybir.AxisListType.X, op=ADD)
         e_late = held.tile([P, LAST, PACK], BF16, align_bytes=64, name="e_late")
-        nc.vector.tensor_copy(e_late[:, :, 0:3], sums[:, 0:3, EARLY:G].rearrange("p t g -> p g t"))
-        add_sums(3, 4, 0, EARLY)
         pick(3, EARLY, G)
+        nc.vector.tensor_copy(e_late[:, :, 0:3], sums[:, 0:3, EARLY:G].rearrange("p t g -> p g t"))
 
         e_early = held.tile([P, EARLY, PACK], BF16, align_bytes=64, name="e_early")
         e_mx = [mx_tiles(128, "e0"), mx_tiles(LAST, "e1"), mx_tiles(LAST, "e2")]
@@ -159,4 +156,4 @@ def tile_attend_hop_kernel(tc, xT, w1, w2, offs, offs2, out):
             multiply(acc[:], w2_mx, e_mx[c], slice(0, g1 - g0))
             result = held.tile([P, g1 - g0], F32, name=f"result{c}")
             nc.scalar.copy(result[:], acc[:])
-            nc.sync.dma_start(out[:, g0:g1], result[:])
+            (nc.scalar if c == 2 else nc.sync).dma_start(out[:, g0:g1], result[:])

@@ -16,8 +16,8 @@ RELU = mybir.ActivationFunctionType.Relu
 
 WINDOW = N + 8
 HALF = N // 2
-LAST = 64
-EARLY = G - LAST
+CHUNK = G // 2
+SPLIT = 96
 
 
 def tile_attend_hop_kernel(tc, xT, w1, w2, offs, offs2, out):
@@ -70,22 +70,25 @@ def tile_attend_hop_kernel(tc, xT, w1, w2, offs, offs2, out):
         x_grouped = held.tile([P, N, PACK], BF16, align_bytes=64, name="x_grouped")
         x_mx = mx_tiles(N, "x")
         for t in range(PACK):
-            nc.vector.tensor_copy(x_grouped[:, :, t], x_raw[t][:].indirect(list1[:]))
+            for a, b in ((0, N),) if t < 3 else ((0, HALF), (HALF, N)):
+                nc.vector.tensor_copy(x_grouped[:, a:b, t], x_raw[t][:].indirect(list1[:, a // 16 : b // 16]))
         for s in range(2):
             cols = slice(s * HALF, (s + 1) * HALF)
             quantize(x_mx[0][:, cols], x_mx[1][:, cols], x_grouped[:, cols, :])
 
         w1_by_t = w1_raw[:].rearrange("p j (m t) -> p t m j", t=PACK)
-        w_grouped = [held.tile([P, P, PACK], BF16, align_bytes=64, name=f"w_grouped{t}") for t in range(PACK)]
         w_mx = [mx_tiles(P, f"w{t}") for t in range(PACK)]
 
         def layer1(t):
+            grouped = held.tile([P, P, PACK], BF16, align_bytes=64, name=f"w_grouped{max(t, 1)}")
             if t == 0:
-                nc.scalar.copy(w_grouped[t][:, 64:], w1_by_t[:, t, 64:])
-                nc.vector.tensor_copy(w_grouped[t][:, :64], w1_by_t[:, t, :64])
+                nc.vector.tensor_copy(grouped[:, :SPLIT], w1_by_t[:, t, :SPLIT])
+                nc.scalar.copy(grouped[:, SPLIT:], w1_by_t[:, t, SPLIT:])
+            elif t == 1:
+                nc.vector.tensor_copy(grouped[:], w1_by_t[:, t])
             else:
-                nc.scalar.copy(w_grouped[t][:], w1_by_t[:, t])
-            quantize(w_mx[t][0][:], w_mx[t][1][:], w_grouped[t][:])
+                nc.scalar.copy(grouped[:], w1_by_t[:, t])
+            quantize(w_mx[t][0][:], w_mx[t][1][:], grouped[:])
             if t == 0:
                 for s in range(2):
                     cols = slice(s * HALF, (s + 1) * HALF)
@@ -101,8 +104,9 @@ def tile_attend_hop_kernel(tc, xT, w1, w2, offs, offs2, out):
                 nc.scalar.activation(h[t][:, 0:N], acc[:], RELU)
 
         picked = held.tile([P, PACK, G, K], F32, name="picked")
-        pairs = held.tile([P, PACK, G, 2], F32, name="pairs")
+        pairs = held.tile([P, PACK - 1, G, 2], F32, name="pairs")
         sums = held.tile([P, PACK, G], F32, name="sums")
+        nc.gpsimd.memset(sums[:, 3, CHUNK:], 0.0)
 
         def pick(t, g0, g1):
             nc.vector.tensor_copy(
@@ -113,47 +117,46 @@ def tile_attend_hop_kernel(tc, xT, w1, w2, offs, offs2, out):
         def add(t, g0, g1):
             nc.gpsimd.tensor_tensor(pairs[:, t, g0:g1, :], picked[:, t, g0:g1, 0:2], picked[:, t, g0:g1, 2:4], ADD)
 
-        def finish(t, g0, g1):
-            nc.gpsimd.tensor_tensor(sums[:, t, g0:g1], pairs[:, t, g0:g1, 0], pairs[:, t, g0:g1, 1], ADD)
+        def finish(t):
+            nc.gpsimd.tensor_tensor(sums[:, t, :], pairs[:, t, :, 0], pairs[:, t, :, 1], ADD)
+
+        def reduce3(to, g0, g1):
+            with nc.allow_low_precision(reason="the engine sums in float32 and rounds once, on the way out"):
+                nc.vector.tensor_reduce(out=to, in_=picked[:, 3, g0:g1, :], axis=mybir.AxisListType.X, op=ADD)
 
         layer1(0)
         layer1(1)
-        for t in range(3):
-            for g0 in (0, 128):
-                pick(t, g0, g0 + 128)
-                if t == 2:
-                    add(t, g0, g0 + 128)
-            if t < 2:
-                add(t, 0, G)
-            finish(t, 0, G)
-            if t < 2:
-                layer1(t + 2)
+        layer1(2)
+        layer1(3)
         w2_grouped = held.tile([P, M, PACK], BF16, align_bytes=64, name="w2_grouped")
         w2_mx = mx_tiles(M, "w2")
         nc.scalar.copy(w2_grouped[:], w2_raw[:].rearrange("p j m -> p m j"))
-        quantize(w2_mx[0][:], w2_mx[1][:], w2_grouped[:])
-        pick(3, 0, 128)
-        add(3, 0, 128)
-        finish(3, 0, 128)
-        pick(3, 128, EARLY)
-        nc.vector.tensor_reduce(out=sums[:, 3, 128:EARLY], in_=picked[:, 3, 128:EARLY, :], axis=mybir.AxisListType.X, op=ADD)
-        e_late = held.tile([P, LAST, PACK], BF16, align_bytes=64, name="e_late")
-        pick(3, EARLY, G)
-        nc.vector.tensor_copy(e_late[:, :, 0:3], sums[:, 0:3, EARLY:G].rearrange("p t g -> p g t"))
+        e = [held.tile([P, CHUNK, PACK], BF16, align_bytes=64, name=f"e{c}") for c in range(2)]
+        e_mx = [mx_tiles(CHUNK, f"e{c}") for c in range(2)]
 
-        e_early = held.tile([P, EARLY, PACK], BF16, align_bytes=64, name="e_early")
-        e_mx = [mx_tiles(128, "e0"), mx_tiles(LAST, "e1"), mx_tiles(LAST, "e2")]
-        parts = ((0, 128), (128, EARLY), (EARLY, G))
-        for g0, g1 in parts[:2]:
-            nc.scalar.copy(e_early[:, g0:g1, :], sums[:, :, g0:g1].rearrange("p t g -> p g t"))
-        quantize(e_mx[0][0][:], e_mx[0][1][:], e_early[:, 0:128, :])
-        with nc.allow_low_precision(reason="the engine sums in float32 and rounds once, on the way out"):
-            nc.vector.tensor_reduce(out=e_late[:, :, 3], in_=picked[:, 3, EARLY:G, :], axis=mybir.AxisListType.X, op=ADD)
-        quantize(e_mx[1][0][:], e_mx[1][1][:], e_early[:, 128:EARLY, :])
-        quantize(e_mx[2][0][:], e_mx[2][1][:], e_late[:])
-        for c, (g0, g1) in enumerate(parts):
-            acc = psum.tile([P, g1 - g0], F32, name=f"out_bank{c}")
-            multiply(acc[:], w2_mx, e_mx[c], slice(0, g1 - g0))
-            result = held.tile([P, g1 - g0], F32, name=f"result{c}")
+        def group(c):
+            nc.scalar.copy(e[c][:], sums[:, :, c * CHUNK : (c + 1) * CHUNK].rearrange("p t g -> p g t"))
+
+        for t in range(3):
+            for g0 in (0, CHUNK):
+                pick(t, g0, g0 + CHUNK)
+                if t == 2:
+                    add(t, g0, g0 + CHUNK)
+            if t < 2:
+                add(t, 0, G)
+            finish(t)
+        group(1)
+        pick(3, 0, CHUNK)
+        reduce3(sums[:, 3, 0:CHUNK], 0, CHUNK)
+        group(0)
+        pick(3, CHUNK, G)
+        quantize(e_mx[0][0][:], e_mx[0][1][:], e[0][:])
+        reduce3(e[1][:, :, 3], CHUNK, G)
+        quantize(w2_mx[0][:], w2_mx[1][:], w2_grouped[:])
+        quantize(e_mx[1][0][:], e_mx[1][1][:], e[1][:])
+        for c in range(2):
+            acc = psum.tile([P, CHUNK], F32, name=f"out_bank{c}")
+            multiply(acc[:], w2_mx, e_mx[c], slice(0, CHUNK))
+            result = held.tile([P, CHUNK], F32, name=f"result{c}")
             nc.scalar.copy(result[:], acc[:])
-            (nc.scalar if c == 2 else nc.sync).dma_start(out[:, g0:g1], result[:])
+            (nc.sync, nc.scalar)[c].dma_start(out[:, c * CHUNK : (c + 1) * CHUNK], result[:])

import concourse.mybir as mybir

P = 128
PACK = 4
N, T, D, H, M, G, K = 512, 2048, 512, 512, 128, 256, 4
FLOPS = 2 * D * H * N + 2 * H * M * G

F32 = mybir.dt.float32
BF16 = mybir.dt.bfloat16
U32 = mybir.dt.uint32
U16 = mybir.dt.uint16
U8 = mybir.dt.uint8
FP8X4 = mybir.dt.float8_e4m3fn_x4
ADD = mybir.AluOpType.add
RELU = mybir.ActivationFunctionType.Relu

WINDOW = N + 8
HALF = N // 2
CHUNK = G // 2
SPLIT = 96


def tile_attend_hop_kernel(tc, xT, w1, w2, offs, offs2, out):
    nc = tc.nc
    with (
        tc.tile_pool(name="held", bufs=1) as held,
        tc.psum_pool(name="psum", bufs=1) as psum,
    ):
        list1 = held.tile([P, N // 16], U16, name="list1")
        list2 = held.tile([P, G * K // 16], U16, name="list2")

        x_rows = xT.rearrange("(p t) n -> t p n", t=PACK)
        x_raw = [held.tile([P, T], F32, name=f"x_raw{t}") for t in range(PACK)]
        w1_raw = held.tile([P, PACK, H], F32, name="w1_raw")
        w2_raw = held.tile([P, PACK, M], F32, name="w2_raw")
        nc.sync.dma_start(x_raw[0][:], x_rows[0])
        nc.sync.dma_start(list1[:], offs)
        nc.sync.dma_start(x_raw[1][:], x_rows[1])
        nc.sync.dma_start(x_raw[2][:], x_rows[2])
        nc.sync.dma_start(x_raw[3][:], x_rows[3])
        nc.sync.dma_start(w1_raw[:], w1.rearrange("(p j) c -> p j c", j=PACK))
        nc.sync.dma_start(list2[:], offs2)
        nc.sync.dma_start(w2_raw[:], w2.rearrange("(p j) m -> p j m", j=PACK))

        h = []
        for t in range(PACK):
            h_t = held.tile([P, WINDOW], F32, name=f"h{t}")
            nc.gpsimd.memset(h_t[:, N:], 0.0)
            h.append(h_t)

        def quantize(codes, scales, grouped):
            nc.vector.quantize_mx(out=codes.bitcast(FP8X4), scales=scales, in_=grouped.rearrange("p n t -> p (n t)"))

        def multiply(acc, w, x, cols):
            nc.tensor.matmul_mx(
                out=acc,
                lhsT=w[0][:].bitcast(FP8X4),
                lhsT_scale=w[1][:],
                rhs=x[0][:, cols].bitcast(FP8X4),
                rhs_scale=x[1][:, cols],
                start=True,
                stop=True,
            )

        def mx_tiles(width, name):
            codes = held.tile([P, width], U32, align_bytes=64, name=f"{name}_codes")
            scales = held.tile([P, width], U8, align_bytes=64, name=f"{name}_scales")
            return codes, scales

        x_grouped = held.tile([P, N, PACK], BF16, align_bytes=64, name="x_grouped")
        x_mx = mx_tiles(N, "x")
        for t in range(PACK):
            for a, b in ((0, N),) if t < 3 else ((0, HALF), (HALF, N)):
                nc.vector.tensor_copy(x_grouped[:, a:b, t], x_raw[t][:].indirect(list1[:, a // 16 : b // 16]))
        for s in range(2):
            cols = slice(s * HALF, (s + 1) * HALF)
            quantize(x_mx[0][:, cols], x_mx[1][:, cols], x_grouped[:, cols, :])

        w1_by_t = w1_raw[:].rearrange("p j (m t) -> p t m j", t=PACK)
        w_mx = [mx_tiles(P, f"w{t}") for t in range(PACK)]

        def layer1(t):
            grouped = held.tile([P, P, PACK], BF16, align_bytes=64, name=f"w_grouped{max(t, 1)}")
            if t == 0:
                nc.vector.tensor_copy(grouped[:, :SPLIT], w1_by_t[:, t, :SPLIT])
                nc.scalar.copy(grouped[:, SPLIT:], w1_by_t[:, t, SPLIT:])
            elif t == 1:
                nc.vector.tensor_copy(grouped[:], w1_by_t[:, t])
            else:
                nc.scalar.copy(grouped[:], w1_by_t[:, t])
            quantize(w_mx[t][0][:], w_mx[t][1][:], grouped[:])
            if t == 0:
                for s in range(2):
                    cols = slice(s * HALF, (s + 1) * HALF)
                    acc = psum.tile([P, HALF], F32, name=f"bank0{s}")
                    multiply(acc[:], w_mx[t], x_mx, cols)
                    if s == 0:
                        nc.scalar.activation(h[t][:, cols], acc[:], RELU)
                    else:
                        nc.vector.tensor_scalar_max(h[t][:, cols], acc[:], 0.0)
            else:
                acc = psum.tile([P, N], F32, name=f"bank{t}")
                multiply(acc[:], w_mx[t], x_mx, slice(0, N))
                nc.scalar.activation(h[t][:, 0:N], acc[:], RELU)

        picked = held.tile([P, PACK, G, K], F32, name="picked")
        pairs = held.tile([P, PACK - 1, G, 2], F32, name="pairs")
        sums = held.tile([P, PACK, G], F32, name="sums")
        nc.gpsimd.memset(sums[:, 3, CHUNK:], 0.0)

        def pick(t, g0, g1):
            nc.vector.tensor_copy(
                picked[:, t, g0:g1, :].rearrange("p g j -> p (g j)"),
                h[t][:].indirect(list2[:, g0 * K // 16 : g1 * K // 16]),
            )

        def add(t, g0, g1):
            nc.gpsimd.tensor_tensor(pairs[:, t, g0:g1, :], picked[:, t, g0:g1, 0:2], picked[:, t, g0:g1, 2:4], ADD)

        def finish(t):
            nc.gpsimd.tensor_tensor(sums[:, t, :], pairs[:, t, :, 0], pairs[:, t, :, 1], ADD)

        def reduce3(to, g0, g1):
            with nc.allow_low_precision(reason="the engine sums in float32 and rounds once, on the way out"):
                nc.vector.tensor_reduce(out=to, in_=picked[:, 3, g0:g1, :], axis=mybir.AxisListType.X, op=ADD)

        layer1(0)
        layer1(1)
        layer1(2)
        layer1(3)
        w2_grouped = held.tile([P, M, PACK], BF16, align_bytes=64, name="w2_grouped")
        w2_mx = mx_tiles(M, "w2")
        nc.scalar.copy(w2_grouped[:], w2_raw[:].rearrange("p j m -> p m j"))
        e = [held.tile([P, CHUNK, PACK], BF16, align_bytes=64, name=f"e{c}") for c in range(2)]
        e_mx = [mx_tiles(CHUNK, f"e{c}") for c in range(2)]

        def group(c):
            nc.scalar.copy(e[c][:], sums[:, :, c * CHUNK : (c + 1) * CHUNK].rearrange("p t g -> p g t"))

        for t in range(3):
            for g0 in (0, CHUNK):
                pick(t, g0, g0 + CHUNK)
                if t == 2:
                    add(t, g0, g0 + CHUNK)
            if t < 2:
                add(t, 0, G)
            finish(t)
        group(1)
        pick(3, 0, CHUNK)
        reduce3(sums[:, 3, 0:CHUNK], 0, CHUNK)
        group(0)
        pick(3, CHUNK, G)
        quantize(e_mx[0][0][:], e_mx[0][1][:], e[0][:])
        reduce3(e[1][:, :, 3], CHUNK, G)
        quantize(w2_mx[0][:], w2_mx[1][:], w2_grouped[:])
        quantize(e_mx[1][0][:], e_mx[1][1][:], e[1][:])
        for c in range(2):
            acc = psum.tile([P, CHUNK], F32, name=f"out_bank{c}")
            multiply(acc[:], w2_mx, e_mx[c], slice(0, CHUNK))
            result = held.tile([P, CHUNK], F32, name=f"result{c}")
            nc.scalar.copy(result[:], acc[:])
            (nc.sync, nc.scalar)[c].dma_start(out[:, c * CHUNK : (c + 1) * CHUNK], result[:])
